import numpy as np, ml_dtypes
CORES = [12,28,60,100,156,228]
N = 6
R, TK = 32, 128
WID = [48,16,64,128,32,80]
def setup_inputs(rng):
    u = (rng.standard_normal((N, 128, R), dtype=np.float32) / 11).astype(ml_dtypes.bfloat16)
    return {"x": rng.standard_normal((N, 128, TK), dtype=np.float32).astype(ml_dtypes.bfloat16), "u": u, "ut": u.transpose(0, 2, 1).copy(), "vt": rng.standard_normal((N, R, 128), dtype=np.float32).astype(ml_dtypes.bfloat16)}
def setup_inputs_big(rng):
    d = setup_inputs(rng)
    for k in ("x", "u", "ut", "vt"): d[k] = (d[k].astype(np.float32) * 1024.0).astype(d[k].dtype)
    return d
def setup_inputs_small(rng):
    d = setup_inputs(rng)
    for k in ("x", "u", "ut", "vt"): d[k] = (d[k].astype(np.float32) * (1 / 1024.0)).astype(d[k].dtype)
    return d
def setup_inputs_apart(rng):
    d = setup_inputs(rng)
    f = (10.0 ** rng.permutation(np.linspace(-1.5, 1.5, N))).astype(np.float32).reshape(N, 1, 1)
    for k in ("x", "u", "ut", "vt"): d[k] = (d[k].astype(np.float32) * f).astype(d[k].dtype)
    return d
def tie_inputs(x):
    x = dict(x)
    x["ut"] = x["u"].transpose(0, 2, 1).copy()
    return x
def whole(x, u, ut, vt):
    X, U, VT = x.astype(np.float64), u.astype(np.float64), vt.astype(np.float64)
    y = np.stack([sum(VT[j].T @ (U[j].T @ X[r]) for j in range(N)) for r in range(N)])
    return {"y": y.astype(ml_dtypes.bfloat16 if x.dtype != np.float64 else np.float64)}
def reference(x, u, ut, vt):
    o = whole(x, u, ut, vt)["y"].copy()
    for r in range(N):
        o[r][:, WID[r]:] = np.nan
    return {"y": o}

@@ -1,0 +1,123 @@
+from concourse.bass import DstId, RemoteDMATransfer
+
+N = 6
+SIM_CORES = 256
+
+SCRATCH = {
+    "ut_sb": ("sbuf", [32, 128], "bfloat16"),
+    "vt_sb": ("sbuf", [32, 128], "bfloat16"),
+    "x_sb": ("sbuf", [128, 128], "bfloat16"),
+    "p_sb": ("sbuf", [128, 128], "bfloat16"),
+    "rel": ("sbuf", [128, 128], "bfloat16"),
+    "land": ("sbuf", [128, N * 128], "bfloat16"),
+    "y_sb": ("sbuf", [128, 128], "bfloat16"),
+    "p_ps": ("psum", [128, 512], "float32"),
+    "y_ps": ("psum", [128, 512], "float32"),
+}
+SEMAPHORES = ["ld_uv", "ld_x", "mm1", "pcopy", "rel_in", "sent", "mm2", "ycopy", "st"] + ["arr%d" % s for s in range(N)]
+
+
+def _count(mask):
+    return sum((mask >> i) & 1 for i in range(16))
+
+
+def _routes(T, topo):
+    cores = list(T.cores)
+    into = [{} for _ in cores]
+    via = {}
+    for s, cs in enumerate(cores):
+        chipmates = [c for c in range(SIM_CORES) if c not in cores
+                     and topo.host(c) == topo.host(cs) and topo.chip(c) == topo.chip(cs)]
+        out_of, taken = {}, []
+        for d, cd in enumerate(cores):
+            if d == s or topo.may_write(cs, cd):
+                continue
+            able = [c for c in chipmates if c not in taken and topo.may_write(c, cd)]
+            able.sort(key=lambda c: (into[d].get(topo.die(c), 0), out_of.get(topo.die(c), 0), c))
+            h = able[0]
+            taken.append(h)
+            out_of[topo.die(h)] = out_of.get(topo.die(h), 0) + 1
+            into[d][topo.die(h)] = into[d].get(topo.die(h), 0) + 1
+            via[(s, d)] = h
+    return via
+
+
+def _dst(topo, dst, src):
+    rid, pid = topo.addr(dst, src)
+    return DstId(rid=rid, pnc=pid)
+
+
+def _common_mask(topo, src, dsts):
+    m = topo.mask(src, dsts[0])
+    for d in dsts[1:]:
+        m &= topo.mask(src, d)
+    return m
+
+
+def rank_program(g, core, T, topo):
+    cores = list(T.cores)
+    via = _routes(T, topo)
+    rank = T.rank_of(core)
+
+    if rank is None:
+        jobs = [(s, d) for (s, d), h in via.items() if h == core]
+        if not jobs:
+            return
+        (s, d), = jobs
+        helpers = [via[k] for k in sorted(via) if k[0] == s]
+        g.wait_ge(T.sem.rel_in, _count(_common_mask(topo, cores[s], helpers)))
+        rid, pid = topo.addr(cores[d], core)
+        m = topo.mask(core, cores[d])
+        g.remote_dma(T.land[:, s * 128:(s + 1) * 128], T.rel[:], T.sem["arr%d" % s], T.sem.sent, pid, rid, m)
+        g.wait_ge(T.sem.sent, _count(m))
+        return
+
+    w = T.tables["WID"][rank]
+    direct = [d for d in range(N) if d != rank and (rank, d) not in via]
+    helpers = [via[k] for k in sorted(via) if k[0] == rank]
+
+    g.sync.dma_start(T.ut_sb[:], T.ut[:]).then_inc(T.sem.ld_uv, 16)
+    g.scalar.dma_start(T.vt_sb[:], T.vt[:]).then_inc(T.sem.ld_uv, 16)
+    g.sync.dma_start(T.x_sb[:, 0:w], T.x[:, 0:w]).then_inc(T.sem.ld_x, 16)
+
+    g.tensor.wait_ge(T.sem.ld_uv, 32)
+    g.tensor.matmul(T.p_ps[:, 0:128], T.ut_sb[:], T.vt_sb[:], start=True, stop=True).then_inc(T.sem.mm1, 1)
+    g.vector.wait_ge(T.sem.mm1, 1)
+    g.vector.tensor_copy(T.p_sb[:], T.p_ps[:, 0:128]).then_inc(T.sem.pcopy, 1)
+
+    g.wait_ge(T.sem.pcopy, 1)
+    sent = 0
+    if helpers:
+        m = _common_mask(topo, core, helpers)
+        g.remote_dma_fused([RemoteDMATransfer(dst_ids=[_dst(topo, h, core) for h in helpers], dma_engine_mask=m,
+                                              remote_sem=T.sem.rel_in, srcs=[T.p_sb[:]],
+                                              dsts=[T.rel[:] for _ in helpers])], local_sem=T.sem.sent)
+        sent += _count(m)
+    if direct:
+        m = _common_mask(topo, core, [cores[d] for d in direct])
+        g.remote_dma_fused([RemoteDMATransfer(dst_ids=[_dst(topo, cores[d], core) for d in direct], dma_engine_mask=m,
+                                              remote_sem=T.sem["arr%d" % rank], srcs=[T.p_sb[:]],
+                                              dsts=[T.land[:, rank * 128:(rank + 1) * 128] for _ in direct])],
+                           local_sem=T.sem.sent)
+        sent += _count(m)
+
+    g.tensor.wait_ge(T.sem.pcopy, 1)
+    g.tensor.wait_ge(T.sem.ld_x, 16)
+    g.tensor.matmul(T.y_ps[:, 0:w], T.p_sb[:], T.x_sb[:, 0:w], start=True, stop=False)
+    order = direct + [s for s in range(N) if (s, rank) in via]
+    for i, s in enumerate(order):
+        if (s, rank) in via:
+            n = _count(topo.mask(via[(s, rank)], core))
+        else:
+            n = _count(_common_mask(topo, cores[s], [cores[d] for d in range(N) if d != s and (s, d) not in via]))
+        g.tensor.wait_ge(T.sem["arr%d" % s], n)
+        mm = g.tensor.matmul(T.y_ps[:, 0:w], T.land[:, s * 128:(s + 1) * 128], T.x_sb[:, 0:w],
+                             start=False, stop=(i == len(order) - 1))
+    mm.then_inc(T.sem.mm2, 1)
+
+    g.vector.wait_ge(T.sem.mm2, 1)
+    g.vector.tensor_copy(T.y_sb[:, 0:w], T.y_ps[:, 0:w]).then_inc(T.sem.ycopy, 1)
+    g.sync.wait_ge(T.sem.ycopy, 1)
+    g.sync.dma_start(T.y[:, 0:w], T.y_sb[:, 0:w]).then_inc(T.sem.st, 16)
+    g.sync.wait_ge(T.sem.st, 16)
+    g.wait_ge(T.sem.sent, sent)

@@ -2,19 +2,34 @@ from concourse.bass import DstId, RemoteDMATransfer
 
 N = 6
 SIM_CORES = 256
+NREL = 4
 
 SCRATCH = {
+    "u_d": ("dram", [128, 32], "bfloat16"),
+    "vt_d": ("dram", [128, 128], "bfloat16"),
+    "rel_u": ("dram", [128, 32], "bfloat16"),
+    "rel_v": ("dram", [128, 128], "bfloat16"),
+    "z_sb": ("sbuf", [96, 128], "bfloat16"),
     "ut_sb": ("sbuf", [32, 128], "bfloat16"),
     "vt_sb": ("sbuf", [32, 128], "bfloat16"),
     "x_sb": ("sbuf", [128, 128], "bfloat16"),
     "p_sb": ("sbuf", [128, 128], "bfloat16"),
-    "rel": ("sbuf", [128, 128], "bfloat16"),
     "land": ("sbuf", [128, N * 128], "bfloat16"),
+    "land_u": ("sbuf", [128, N * 32], "bfloat16"),
+    "land_v": ("sbuf", [128, N * 128], "bfloat16"),
+    "t_sb": ("sbuf", [32, NREL * 128], "bfloat16"),
     "y_sb": ("sbuf", [128, 128], "bfloat16"),
     "p_ps": ("psum", [128, 512], "float32"),
     "y_ps": ("psum", [128, 512], "float32"),
+    "t_ps0": ("psum", [128, 512], "float32"),
+    "t_ps1": ("psum", [128, 512], "float32"),
+    "t_ps2": ("psum", [128, 512], "float32"),
+    "t_ps3": ("psum", [128, 512], "float32"),
 }
-SEMAPHORES = ["ld_uv", "ld_x", "mm1", "pcopy", "rel_in", "sent", "mm2", "ycopy", "st"] + ["arr%d" % s for s in range(N)]
+SEMAPHORES = (["zfill", "ld_ud", "ld_vd", "ld_uv", "ld_x", "mm1", "pcopy", "relu_in", "relv_in", "sent", "mm2", "ycopy",
+               "st"]
+              + ["arr%d" % s for s in range(N)] + ["au%d" % s for s in range(N)] + ["av%d" % s for s in range(N)]
+              + ["tmm%d" % i for i in range(NREL)] + ["tcp%d" % i for i in range(NREL)])
 
 
 def _count(mask):
@@ -54,6 +69,15 @@ def _common_mask(topo, src, dsts):
     return m
 
 
+def _feed_masks(T, topo, via, s):
+    cores = list(T.cores)
+    cs = cores[s]
+    helpers = [via[k] for k in sorted(via) if k[0] == s]
+    on = _common_mask(topo, cs, helpers)
+    off = _common_mask(topo, cs, [c for c in cores if c != cs and topo.may_write(cs, c)])
+    return on & ~off, on
+
+
 def rank_program(g, core, T, topo):
     cores = list(T.cores)
     via = _routes(T, topo)
@@ -64,18 +88,26 @@ def rank_program(g, core, T, topo):
         if not jobs:
             return
         (s, d), = jobs
-        helpers = [via[k] for k in sorted(via) if k[0] == s]
-        g.wait_ge(T.sem.rel_in, _count(_common_mask(topo, cores[s], helpers)))
+        mu, mv = _feed_masks(T, topo, via, s)
         rid, pid = topo.addr(cores[d], core)
         m = topo.mask(core, cores[d])
-        g.remote_dma(T.land[:, s * 128:(s + 1) * 128], T.rel[:], T.sem["arr%d" % s], T.sem.sent, pid, rid, m)
-        g.wait_ge(T.sem.sent, _count(m))
+        g.wait_ge(T.sem.relu_in, _count(mu))
+        g.remote_dma(T.land_u[:, s * 32:(s + 1) * 32], T.rel_u[:], T.sem["au%d" % s], T.sem.sent, pid, rid, m)
+        g.wait_ge(T.sem.relv_in, _count(mv))
+        g.remote_dma(T.land_v[:, s * 128:(s + 1) * 128], T.rel_v[:], T.sem["av%d" % s], T.sem.sent, pid, rid, m)
+        g.wait_ge(T.sem.sent, 2 * _count(m))
         return
 
     w = T.tables["WID"][rank]
     direct = [d for d in range(N) if d != rank and (rank, d) not in via]
     helpers = [via[k] for k in sorted(via) if k[0] == rank]
+    relayed = [s for s in range(N) if (s, rank) in via]
 
+    g.vector.memset(T.z_sb[:], 0.0).then_inc(T.sem.zfill, 1)
+    g.sync.dma_start(T.u_d[:], T.u[:]).then_inc(T.sem.ld_ud, 16)
+    g.scalar.dma_start(T.vt_d[0:32, :], T.vt[:]).then_inc(T.sem.ld_vd, 16)
+    g.scalar.wait_ge(T.sem.zfill, 1)
+    g.scalar.dma_start(T.vt_d[32:128, :], T.z_sb[:]).then_inc(T.sem.ld_vd, 16)
     g.sync.dma_start(T.ut_sb[:], T.ut[:]).then_inc(T.sem.ld_uv, 16)
     g.scalar.dma_start(T.vt_sb[:], T.vt[:]).then_inc(T.sem.ld_uv, 16)
     g.sync.dma_start(T.x_sb[:, 0:w], T.x[:, 0:w]).then_inc(T.sem.ld_x, 16)
@@ -85,34 +117,40 @@ def rank_program(g, core, T, topo):
     g.vector.wait_ge(T.sem.mm1, 1)
     g.vector.tensor_copy(T.p_sb[:], T.p_ps[:, 0:128]).then_inc(T.sem.pcopy, 1)
 
+    mu, mv = _feed_masks(T, topo, via, rank)
+    hid = [_dst(topo, h, core) for h in helpers]
+    g.wait_ge(T.sem.ld_ud, 16)
+    g.remote_dma_fused([RemoteDMATransfer(dst_ids=hid, dma_engine_mask=mu, remote_sem=T.sem.relu_in, srcs=[T.u_d[:]],
+                                          dsts=[T.rel_u[:] for _ in helpers])], local_sem=T.sem.sent)
+    g.wait_ge(T.sem.ld_vd, 32)
+    g.remote_dma_fused([RemoteDMATransfer(dst_ids=hid, dma_engine_mask=mv, remote_sem=T.sem.relv_in, srcs=[T.vt_d[:]],
+                                          dsts=[T.rel_v[:] for _ in helpers])], local_sem=T.sem.sent)
     g.wait_ge(T.sem.pcopy, 1)
-    sent = 0
-    if helpers:
-        m = _common_mask(topo, core, helpers)
-        g.remote_dma_fused([RemoteDMATransfer(dst_ids=[_dst(topo, h, core) for h in helpers], dma_engine_mask=m,
-                                              remote_sem=T.sem.rel_in, srcs=[T.p_sb[:]],
-                                              dsts=[T.rel[:] for _ in helpers])], local_sem=T.sem.sent)
-        sent += _count(m)
-    if direct:
-        m = _common_mask(topo, core, [cores[d] for d in direct])
-        g.remote_dma_fused([RemoteDMATransfer(dst_ids=[_dst(topo, cores[d], core) for d in direct], dma_engine_mask=m,
-                                              remote_sem=T.sem["arr%d" % rank], srcs=[T.p_sb[:]],
-                                              dsts=[T.land[:, rank * 128:(rank + 1) * 128] for _ in direct])],
-                           local_sem=T.sem.sent)
-        sent += _count(m)
+    md = _common_mask(topo, core, [cores[d] for d in direct])
+    g.remote_dma_fused([RemoteDMATransfer(dst_ids=[_dst(topo, cores[d], core) for d in direct], dma_engine_mask=md,
+                                          remote_sem=T.sem["arr%d" % rank], srcs=[T.p_sb[:]],
+                                          dsts=[T.land[:, rank * 128:(rank + 1) * 128] for _ in direct])],
+                       local_sem=T.sem.sent)
+    sent = _count(mu) + _count(mv) + _count(md)
 
     g.tensor.wait_ge(T.sem.pcopy, 1)
     g.tensor.wait_ge(T.sem.ld_x, 16)
     g.tensor.matmul(T.y_ps[:, 0:w], T.p_sb[:], T.x_sb[:, 0:w], start=True, stop=False)
-    order = direct + [s for s in range(N) if (s, rank) in via]
-    for i, s in enumerate(order):
-        if (s, rank) in via:
-            n = _count(topo.mask(via[(s, rank)], core))
-        else:
-            n = _count(_common_mask(topo, cores[s], [cores[d] for d in range(N) if d != s and (s, d) not in via]))
+    for i, s in enumerate(relayed):
+        g.tensor.wait_ge(T.sem["au%d" % s], _count(topo.mask(via[(s, rank)], core)))
+        g.tensor.matmul(T["t_ps%d" % i][0:32, 0:w], T.land_u[:, s * 32:(s + 1) * 32], T.x_sb[:, 0:w],
+                        start=True, stop=True).then_inc(T.sem["tmm%d" % i], 1)
+        g.vector.wait_ge(T.sem["tmm%d" % i], 1)
+        g.vector.tensor_copy(T.t_sb[0:32, i * 128:i * 128 + w], T["t_ps%d" % i][0:32, 0:w]).then_inc(T.sem["tcp%d" % i], 1)
+    for s in direct:
+        n = _count(_common_mask(topo, cores[s], [cores[d] for d in range(N) if d != s and (s, d) not in via]))
         g.tensor.wait_ge(T.sem["arr%d" % s], n)
-        mm = g.tensor.matmul(T.y_ps[:, 0:w], T.land[:, s * 128:(s + 1) * 128], T.x_sb[:, 0:w],
-                             start=False, stop=(i == len(order) - 1))
+        g.tensor.matmul(T.y_ps[:, 0:w], T.land[:, s * 128:(s + 1) * 128], T.x_sb[:, 0:w], start=False, stop=False)
+    for i, s in enumerate(relayed):
+        g.tensor.wait_ge(T.sem["tcp%d" % i], 1)
+        g.tensor.wait_ge(T.sem["av%d" % s], _count(topo.mask(via[(s, rank)], core)))
+        mm = g.tensor.matmul(T.y_ps[:, 0:w], T.land_v[0:32, s * 128:(s + 1) * 128], T.t_sb[0:32, i * 128:i * 128 + w],
+                             start=False, stop=(i == len(relayed) - 1))
     mm.then_inc(T.sem.mm2, 1)
 
     g.vector.wait_ge(T.sem.mm2, 1)

from concourse.bass import DstId, RemoteDMATransfer

N = 6
SIM_CORES = 256
NREL = 4

SCRATCH = {
    "u_d": ("dram", [128, 32], "bfloat16"),
    "vt_d": ("dram", [128, 128], "bfloat16"),
    "rel_u": ("dram", [128, 32], "bfloat16"),
    "rel_v": ("dram", [128, 128], "bfloat16"),
    "z_sb": ("sbuf", [96, 128], "bfloat16"),
    "ut_sb": ("sbuf", [32, 128], "bfloat16"),
    "vt_sb": ("sbuf", [32, 128], "bfloat16"),
    "x_sb": ("sbuf", [128, 128], "bfloat16"),
    "p_sb": ("sbuf", [128, 128], "bfloat16"),
    "land": ("sbuf", [128, N * 128], "bfloat16"),
    "land_u": ("sbuf", [128, N * 32], "bfloat16"),
    "land_v": ("sbuf", [128, N * 128], "bfloat16"),
    "t_sb": ("sbuf", [32, NREL * 128], "bfloat16"),
    "y_sb": ("sbuf", [128, 128], "bfloat16"),
    "p_ps": ("psum", [128, 512], "float32"),
    "y_ps": ("psum", [128, 512], "float32"),
    "t_ps0": ("psum", [128, 512], "float32"),
    "t_ps1": ("psum", [128, 512], "float32"),
    "t_ps2": ("psum", [128, 512], "float32"),
    "t_ps3": ("psum", [128, 512], "float32"),
}
SEMAPHORES = (["zfill", "ld_ud", "ld_vd", "ld_uv", "ld_x", "mm1", "pcopy", "relu_in", "relv_in", "sent", "mm2", "ycopy",
               "st"]
              + ["arr%d" % s for s in range(N)] + ["au%d" % s for s in range(N)] + ["av%d" % s for s in range(N)]
              + ["tmm%d" % i for i in range(NREL)] + ["tcp%d" % i for i in range(NREL)])


def _count(mask):
    return sum((mask >> i) & 1 for i in range(16))


def _routes(T, topo):
    cores = list(T.cores)
    into = [{} for _ in cores]
    via = {}
    for s, cs in enumerate(cores):
        chipmates = [c for c in range(SIM_CORES) if c not in cores
                     and topo.host(c) == topo.host(cs) and topo.chip(c) == topo.chip(cs)]
        out_of, taken = {}, []
        for d, cd in enumerate(cores):
            if d == s or topo.may_write(cs, cd):
                continue
            able = [c for c in chipmates if c not in taken and topo.may_write(c, cd)]
            able.sort(key=lambda c: (into[d].get(topo.die(c), 0), out_of.get(topo.die(c), 0), c))
            h = able[0]
            taken.append(h)
            out_of[topo.die(h)] = out_of.get(topo.die(h), 0) + 1
            into[d][topo.die(h)] = into[d].get(topo.die(h), 0) + 1
            via[(s, d)] = h
    return via


def _dst(topo, dst, src):
    rid, pid = topo.addr(dst, src)
    return DstId(rid=rid, pnc=pid)


def _common_mask(topo, src, dsts):
    m = topo.mask(src, dsts[0])
    for d in dsts[1:]:
        m &= topo.mask(src, d)
    return m


def _feed_masks(T, topo, via, s):
    cores = list(T.cores)
    cs = cores[s]
    helpers = [via[k] for k in sorted(via) if k[0] == s]
    on = _common_mask(topo, cs, helpers)
    off = _common_mask(topo, cs, [c for c in cores if c != cs and topo.may_write(cs, c)])
    return on & ~off, on


def rank_program(g, core, T, topo):
    cores = list(T.cores)
    via = _routes(T, topo)
    rank = T.rank_of(core)

    if rank is None:
        jobs = [(s, d) for (s, d), h in via.items() if h == core]
        if not jobs:
            return
        (s, d), = jobs
        mu, mv = _feed_masks(T, topo, via, s)
        rid, pid = topo.addr(cores[d], core)
        m = topo.mask(core, cores[d])
        g.wait_ge(T.sem.relu_in, _count(mu))
        g.remote_dma(T.land_u[:, s * 32:(s + 1) * 32], T.rel_u[:], T.sem["au%d" % s], T.sem.sent, pid, rid, m)
        g.wait_ge(T.sem.relv_in, _count(mv))
        g.remote_dma(T.land_v[:, s * 128:(s + 1) * 128], T.rel_v[:], T.sem["av%d" % s], T.sem.sent, pid, rid, m)
        g.wait_ge(T.sem.sent, 2 * _count(m))
        return

    w = T.tables["WID"][rank]
    direct = [d for d in range(N) if d != rank and (rank, d) not in via]
    helpers = [via[k] for k in sorted(via) if k[0] == rank]
    relayed = [s for s in range(N) if (s, rank) in via]

    g.vector.memset(T.z_sb[:], 0.0).then_inc(T.sem.zfill, 1)
    g.sync.dma_start(T.u_d[:], T.u[:]).then_inc(T.sem.ld_ud, 16)
    g.scalar.dma_start(T.vt_d[0:32, :], T.vt[:]).then_inc(T.sem.ld_vd, 16)
    g.scalar.wait_ge(T.sem.zfill, 1)
    g.scalar.dma_start(T.vt_d[32:128, :], T.z_sb[:]).then_inc(T.sem.ld_vd, 16)
    g.sync.dma_start(T.ut_sb[:], T.ut[:]).then_inc(T.sem.ld_uv, 16)
    g.scalar.dma_start(T.vt_sb[:], T.vt[:]).then_inc(T.sem.ld_uv, 16)
    g.sync.dma_start(T.x_sb[:, 0:w], T.x[:, 0:w]).then_inc(T.sem.ld_x, 16)

    g.tensor.wait_ge(T.sem.ld_uv, 32)
    g.tensor.matmul(T.p_ps[:, 0:128], T.ut_sb[:], T.vt_sb[:], start=True, stop=True).then_inc(T.sem.mm1, 1)
    g.vector.wait_ge(T.sem.mm1, 1)
    g.vector.tensor_copy(T.p_sb[:], T.p_ps[:, 0:128]).then_inc(T.sem.pcopy, 1)

    mu, mv = _feed_masks(T, topo, via, rank)
    hid = [_dst(topo, h, core) for h in helpers]
    g.wait_ge(T.sem.ld_ud, 16)
    g.remote_dma_fused([RemoteDMATransfer(dst_ids=hid, dma_engine_mask=mu, remote_sem=T.sem.relu_in, srcs=[T.u_d[:]],
                                          dsts=[T.rel_u[:] for _ in helpers])], local_sem=T.sem.sent)
    g.wait_ge(T.sem.ld_vd, 32)
    g.remote_dma_fused([RemoteDMATransfer(dst_ids=hid, dma_engine_mask=mv, remote_sem=T.sem.relv_in, srcs=[T.vt_d[:]],
                                          dsts=[T.rel_v[:] for _ in helpers])], local_sem=T.sem.sent)
    g.wait_ge(T.sem.pcopy, 1)
    md = _common_mask(topo, core, [cores[d] for d in direct])
    g.remote_dma_fused([RemoteDMATransfer(dst_ids=[_dst(topo, cores[d], core) for d in direct], dma_engine_mask=md,
                                          remote_sem=T.sem["arr%d" % rank], srcs=[T.p_sb[:]],
                                          dsts=[T.land[:, rank * 128:(rank + 1) * 128] for _ in direct])],
                       local_sem=T.sem.sent)
    sent = _count(mu) + _count(mv) + _count(md)

    g.tensor.wait_ge(T.sem.pcopy, 1)
    g.tensor.wait_ge(T.sem.ld_x, 16)
    g.tensor.matmul(T.y_ps[:, 0:w], T.p_sb[:], T.x_sb[:, 0:w], start=True, stop=False)
    for i, s in enumerate(relayed):
        g.tensor.wait_ge(T.sem["au%d" % s], _count(topo.mask(via[(s, rank)], core)))
        g.tensor.matmul(T["t_ps%d" % i][0:32, 0:w], T.land_u[:, s * 32:(s + 1) * 32], T.x_sb[:, 0:w],
                        start=True, stop=True).then_inc(T.sem["tmm%d" % i], 1)
        g.vector.wait_ge(T.sem["tmm%d" % i], 1)
        g.vector.tensor_copy(T.t_sb[0:32, i * 128:i * 128 + w], T["t_ps%d" % i][0:32, 0:w]).then_inc(T.sem["tcp%d" % i], 1)
    for s in direct:
        n = _count(_common_mask(topo, cores[s], [cores[d] for d in range(N) if d != s and (s, d) not in via]))
        g.tensor.wait_ge(T.sem["arr%d" % s], n)
        g.tensor.matmul(T.y_ps[:, 0:w], T.land[:, s * 128:(s + 1) * 128], T.x_sb[:, 0:w], start=False, stop=False)
    for i, s in enumerate(relayed):
        g.tensor.wait_ge(T.sem["tcp%d" % i], 1)
        g.tensor.wait_ge(T.sem["av%d" % s], _count(topo.mask(via[(s, rank)], core)))
        mm = g.tensor.matmul(T.y_ps[:, 0:w], T.land_v[0:32, s * 128:(s + 1) * 128], T.t_sb[0:32, i * 128:i * 128 + w],
                             start=False, stop=(i == len(relayed) - 1))
    mm.then_inc(T.sem.mm2, 1)

    g.vector.wait_ge(T.sem.mm2, 1)
    g.vector.tensor_copy(T.y_sb[:, 0:w], T.y_ps[:, 0:w]).then_inc(T.sem.ycopy, 1)
    g.sync.wait_ge(T.sem.ycopy, 1)
    g.sync.dma_start(T.y[:, 0:w], T.y_sb[:, 0:w]).then_inc(T.sem.st, 16)
    g.sync.wait_ge(T.sem.st, 16)
    g.wait_ge(T.sem.sent, sent)
